import numpy as np
import ml_dtypes


def mxq(x, axis, fmt="e4m3"):
    dtype, down = {"e4m3": (ml_dtypes.float8_e4m3fn, 7), "e5m2": (ml_dtypes.float8_e5m2, 14)}[fmt]
    v = np.moveaxis(np.asarray(x, np.float32).astype(ml_dtypes.bfloat16).astype(np.float64), axis, -1)
    blocks = v.reshape(v.shape[:-1] + (-1, 32))
    amax = np.abs(blocks).max(-1, keepdims=True)
    byte = np.maximum(np.where(amax > 0, np.frexp(amax)[1] - 1 + 127, 0) - down, 1)
    scale = np.exp2(byte - 127.0)
    codes = (blocks / scale).astype(np.float32).astype(dtype).astype(np.float64)
    return np.moveaxis((codes * scale).reshape(v.shape), -1, axis)


WIDE = False


def mx_kscale(k):
    if not WIDE:
        return np.ones(k)
    levels = np.array([10, -10, 5, -5, 0])
    if k % 512:
        return np.exp2(np.random.permutation(np.resize(levels, k // 32))).repeat(32)
    a = np.empty((k // 512, 16))
    for p in range(k // 512):
        a[p, :8] = np.random.permutation(np.resize(levels, 8))
        for g in range(8):
            far = levels[np.abs(levels - a[p, g]) >= 10]
            a[p, g + 8] = far[np.random.randint(len(far))]
    return np.exp2(a.ravel()).repeat(32)


def f64(x):
    return np.asarray(x).astype(np.float64)


def striped8(idx):
    return np.asarray(idx).reshape(8, -1, 16).transpose(0, 2, 1).reshape(128, -1).astype(np.uint16)


def unstriped8(offs):
    return offs.reshape(8, 16, -1).transpose(0, 2, 1).reshape(8, -1).astype(np.int64)


def pick8(x, idx, run):
    r = np.arange(len(x))
    return x[r[:, None], idx[r % (8 * run) // run]]


E2M1 = np.array([0.0, 0.5, 1.0, 1.5, 2.0, 3.0, 4.0, 6.0, -0.0, -0.5, -1.0, -1.5, -2.0, -3.0, -4.0, -6.0])


def pack_weight(w, fmt):
    k, n = w.shape
    w = f64(np.asarray(w, np.float32).astype(ml_dtypes.bfloat16)).reshape(k // 32, 32, n)
    amax = np.abs(w).max(1)
    if fmt == "e4m3":
        byte = np.frexp(amax)[1] - 1 + 127 - 7
    else:
        mant, ex = np.frexp(amax / 6.0)
        byte = np.where(mant > 0.5, ex, ex - 1) + 127
    byte = np.clip(np.where(amax > 0, byte, 1), 1, 254)
    scaled = (w * np.exp2(127.0 - byte)[:, None, :]).reshape(k, n).astype(np.float32)
    by_word = np.ascontiguousarray(scaled.reshape(k // 512, 128, 4, n).transpose(0, 1, 3, 2))
    if fmt == "e4m3":
        words = by_word.astype(ml_dtypes.float8_e4m3fn).view(np.uint8)
    else:
        c = by_word.astype(ml_dtypes.float4_e2m1fn).view(np.uint8) & 0xF
        words = (c[..., 0::2] | (c[..., 1::2] << 4)).reshape(k // 512, 128, 2 * n)
    return np.ascontiguousarray(words), np.ascontiguousarray(byte.astype(np.uint8).reshape(k // 512, 16, n))


def unpack_weight(words, scales, fmt):
    g, _, n = scales.shape
    words = np.ascontiguousarray(words).reshape(g, 128, n, -1)
    if fmt == "e4m3":
        vals = words.view(ml_dtypes.float8_e4m3fn).astype(np.float64)
    else:
        nib = np.empty((g, 128, n, 4), np.uint8)
        nib[..., 0::2] = words & 0xF
        nib[..., 1::2] = words >> 4
        vals = E2M1[nib]
    vals = vals * np.repeat(np.exp2(scales.astype(np.float64) - 127.0), 8, axis=1)[..., None]
    return vals.transpose(0, 1, 3, 2).reshape(g * 512, n)


D, V, Q, I = 512, 2048, 128, 512


def setup_inputs():
    n = np.random.standard_normal
    idx = np.stack([np.random.permutation(V)[:I] for _ in range(8)])
    fd = mx_kscale(D)
    vocp = pack_weight(n((D, V)) / fd[:, None], "e2m1")
    return {
        "hid": (n((D, Q)) * 1.0 / np.sqrt(D) * fd[:, None]).astype(np.float32),
        "voc_words": vocp[0],
        "voc_scales": vocp[1],
        "th": (np.random.uniform(0.0003, 0.001, (Q, 1))).astype(np.float32),
        "sw": (np.random.uniform(0.5, 2.0, (1, I))).astype(np.float32),
        "old": (0.5 * n((Q, V))).astype(np.float32),
        "offs": striped8(idx),
    }


def reference(hid, voc_words, voc_scales, th, sw, old, offs):
    idx = unstriped8(offs)
    vocu = unpack_weight(voc_words, voc_scales, "e2m1")
    hidq = mxq(f64(hid), 0, "e4m3")
    a = hidq.T @ vocu
    m1 = np.max(a, axis=1, keepdims=True)
    p = np.exp(a - m1)
    z = np.sum(p, axis=1, keepdims=True)
    px = np.exp(pick8(a, idx, 16) - m1)
    dpx = f64(sw) / (px + z * f64(th)) - f64(sw) * px / np.square(px + z * f64(th))
    dz = np.sum(f64(sw) * px / np.square(px + z * f64(th)) * (-1.0), axis=1, keepdims=True) * f64(th)
    e1 = dpx * px
    s1 = np.zeros((Q, V))
    s1[np.arange(Q)[:, None], idx[np.arange(Q) % 128 // 16]] = e1
    da = dz * p + s1
    y = da * 2.0 + f64(old)
    return y

@@ -1,0 +1,184 @@
+from contextlib import ExitStack
+
+import concourse.mybir as mybir
+
+D, V, Q, I = 512, 2048, 128, 512
+FLOPS = 2 * D * V * Q
+
+F32 = mybir.dt.float32
+BF16 = mybir.dt.bfloat16
+I32 = mybir.dt.int32
+U32 = mybir.dt.uint32
+U16 = mybir.dt.uint16
+U8 = mybir.dt.uint8
+FP8X4 = mybir.dt.float8_e4m3fn_x4
+FP4X4 = mybir.dt.float4_e2m1fn_x4
+ALU = mybir.AluOpType
+ACT = mybir.ActivationFunctionType
+AX = mybir.AxisListType
+
+P = 128
+NB = 4
+W = V // NB
+LOG_SLOPE = 11629080.0 / 2.0**47
+LOG_SHIFT = 88.0
+TH_FLOOR = 2.0**-100
+LOG_DEN = 2520
+LOG_POLY = (-252, 2800, -14175, 43200, -88200, 127008, -132300, 100800, -56700, 25200, -7381)
+NT = len(LOG_POLY) - 1
+G_PIECES = ((0, 192), (192, 512), (512, 1024))
+
+
+def tile_attend_bpresence_heads_kernel(tc, hid, voc_words, voc_scales, th, sw, old, offs, out):
+    nc = tc.nc
+    with ExitStack() as ctx:
+        sb = ctx.enter_context(tc.tile_pool(name="sb", bufs=1))
+        ps = ctx.enter_context(tc.psum_pool(name="ps", bufs=1))
+
+        hraw = sb.tile([P, 4, Q], F32, name="hraw", tag="early_a", align_bytes=64)
+        nc.sync.dma_start(out=hraw[:], in_=hid.rearrange("(p j) q -> p j q", j=4))
+        planes = sb.tile([P, V], U8, name="planes", align_bytes=64)
+        nc.gpsimd.memset(planes[:].bitcast(I32), 0)
+        words = []
+        for h in range(2):
+            wt = sb.tile([P, V], U8, name="words%d" % h, align_bytes=64)
+            words.append(wt)
+        nc.sync.dma_start(out=words[0][:].bitcast(I32), in_=voc_words[0][:, 0:V].bitcast(I32))
+        for g in range(4):
+            nc.sync.dma_start(out=planes[32 * g : 32 * g + 4, :].bitcast(I32), in_=voc_scales[0][4 * g : 4 * g + 4, :].bitcast(I32))
+        nc.sync.dma_start(out=words[1][:].bitcast(I32), in_=voc_words[0][:, V : 2 * V].bitcast(I32))
+        offsets = sb.tile([P, I // 16], U16, name="offsets")
+        nc.sync.dma_start(offsets[:], offs)
+        th_raw = sb.tile([P, 1], F32, name="th_raw")
+        nc.sync.dma_start(out=th_raw[:], in_=th)
+
+        consts = sb.tile([P, 1], F32, name="consts")
+        nc.vector.memset(consts[:], 0.5)
+        c_half = consts[:, 0:1]
+        warm = sb.tile([P, 1], F32, name="warm")
+        nc.scalar.activation(warm[:], c_half, ACT.Exp)
+        addend = sb.tile([P, 2 * NT + 1], F32, name="addend")
+        factor = sb.tile([P, 2 * NT + 1], F32, name="factor")
+        nc.vector.memset(addend[:, 0 : 2 * NT], 0.0)
+        for j, c in enumerate(LOG_POLY[1:]):
+            nc.vector.memset(addend[:, 2 * j + 1 : 2 * j + 2], float(c))
+        nc.vector.tensor_scalar(factor[:, 2 * NT : 2 * NT + 1], c_half, -1.0 / LOG_DEN, None, ALU.mult)
+        px = sb.tile([P, I], F32, name="px")
+        c_shift = px[:, I - 1 : I]
+        nc.vector.memset(c_shift, LOG_SHIFT)
+        nc.vector.memset(px[:, 0:1], 1.0)
+        f = sb.tile([P, NB], F32, name="f")
+        nc.gpsimd.memset(f[:, NB - 2 : NB], 1.0)
+        s1 = sb.tile([P, V], F32, name="s1")
+        nc.gpsimd.memset(s1[:, 0 : 2 * W], 0.0)
+        nc.vector.memset(s1[:, 2 * W : 3 * W], 0.0)
+        nc.vector.memset(s1[:, 3 * W : V], 0.0)
+
+        grouped = sb.tile([P, Q, 4], BF16, name="grouped", tag="early_b", align_bytes=64)
+        nc.vector.tensor_copy(
+            out=grouped[:].rearrange("p (c i) t -> p c t i", i=4),
+            in_=hraw[:].rearrange("p t (c i) -> p c t i", i=4),
+        )
+        codes = sb.tile([P, Q], U32, name="codes", align_bytes=64)
+        hscale = sb.tile([P, Q], U8, name="hscale", align_bytes=64)
+        nc.vector.quantize_mx(out=codes[:].bitcast(FP8X4), scales=hscale[:], in_=grouped[:].rearrange("p q t -> p (q t)"))
+
+        swb = sb.tile([P, I], F32, name="swb", tag="early_a", align_bytes=64)
+        nc.sync.dma_start(out=swb[:], in_=sw[0].partition_broadcast(P))
+        old_sb = sb.tile([P, V], F32, name="old_sb", tag="early_b", align_bytes=64)
+        nc.sync.dma_start(out=old_sb[:], in_=old)
+
+        thc = sb.tile([P, 2], F32, name="thc")
+        nc.vector.tensor_scalar(thc[:, 0:1], th_raw[:], TH_FLOOR, None, ALU.max)
+        nc.vector.tensor_scalar(thc[:, 1:2], th_raw[:], TH_FLOOR, -2.0, ALU.max, ALU.mult)
+        th1, thm2 = thc[:, 0:1], thc[:, 1:2]
+
+        a = sb.tile([P, V], F32, name="a")
+        p = sb.tile([P, V], F32, name="p")
+        m = sb.tile([P, NB], F32, name="m")
+        nmax = sb.tile([P, 1], F32, name="nmax")
+        z = sb.tile([P, NB], F32, name="z")
+        nm = [f[:, 0:1], f[:, 1:2], z[:, NB - 1 : NB]]
+        unit = [1.0, 1.0, f[:, 2:3]]
+        for b in range(NB):
+            cols = slice(b * W, (b + 1) * W)
+            bank = ps.tile([P, W], F32, name="bank%d" % b)
+            wcol = (b % 2) * 2 * W
+            nc.tensor.matmul_mx(
+                out=bank[:],
+                lhsT=codes[:].bitcast(FP8X4),
+                lhsT_scale=hscale[:],
+                rhs=words[b // 2][:, wcol : wcol + 2 * W].bitcast(FP4X4),
+                rhs_scale=planes[:, cols],
+                start=True,
+                stop=True,
+            )
+            nc.vector.tensor_scalar(a[:, cols], bank[:], 1.0, None, ALU.mult, ALU.max, accum_out=m[:, b : b + 1])
+            if b < NB - 1:
+                nc.gpsimd.tensor_scalar(nm[b], m[:, b : b + 1], -1.0, 0.0, ALU.mult, ALU.add)
+                nc.scalar.activation(p[:, cols], a[:, cols], ACT.Exp, bias=nm[b], scale=unit[b], accum_out=z[:, b : b + 1])
+        nc.vector.tensor_reduce(nmax[:], m[:], AX.X, ALU.max, negate=True)
+        nc.scalar.activation(f[:, 0 : NB - 1], m[:, 0 : NB - 1], ACT.Exp, bias=nmax[:])
+        last = slice((NB - 1) * W, V)
+        nc.scalar.activation(p[:, last], a[:, last], ACT.Exp, bias=nmax[:], scale=px[:, 0:1], accum_out=z[:, NB - 1 : NB])
+
+        H = I // 2
+        ax = sb.tile([P, I], F32, name="ax")
+        nc.vector.tensor_copy(ax[:], a[:].indirect(offsets[:]))
+        hb = sb.tile([P, 1], F32, name="hb")
+        nc.vector.tensor_scalar(hb[:], nmax[:], 0.5, LOG_SHIFT / 2, ALU.mult, ALU.add)
+        junk = sb.tile([P, NB], F32, name="junk")
+        t = sb.tile([P, 1], F32, name="t")
+        halves = (slice(0, H), slice(H, I))
+        nc.scalar.activation(px[:, halves[0]], ax[:, halves[0]], ACT.Exp, bias=nmax[:])
+        nc.vector.scalar_tensor_tensor(junk[:], f[:], th1, z[:], ALU.mult, ALU.mult, accum_out=t[:])
+        nc.scalar.activation(factor[:, 1 : 2 * NT : 2], t[:].bitcast(U32).to_broadcast([P, NT]), ACT.Exp, bias=c_shift, scale=-LOG_SLOPE)
+        nc.vector.tensor_copy(factor[:, 0 : 2 * NT : 2], t[:].to_broadcast([P, NT]))
+        nc.vector.tensor_scalar(addend[:, 2 * NT : 2 * NT + 1], t[:].bitcast(I32), -LOG_SLOPE / 2, hb[:], ALU.mult, ALU.add)
+        nc.scalar.activation(px[:, halves[1]], ax[:, halves[1]], ACT.Exp, bias=nmax[:])
+        rt = sb.tile([P, 1], F32, name="rt")
+        nc.vector.reciprocal(rt[:], t[:])
+        poly = sb.tile([P, 2 * NT + 1], F32, name="poly")
+        nc.vector.tensor_tensor_scan(poly[:], factor[:], addend[:], float(LOG_POLY[0]), ALU.mult, ALU.add)
+        kf = sb.tile([P, NB], F32, name="kf")
+        nc.vector.tensor_scalar(kf[:], f[:], rt[:], thm2, ALU.mult, ALU.mult)
+
+        tq = sb.tile([P, I], F32, name="tq")
+        qq = sb.tile([P, I], F32, name="qq")
+        nn = sb.tile([P, I], F32, name="nn")
+        e1 = sb.tile([P, I], F32, name="e1")
+        s = sb.tile([P, 2], F32, name="s")
+        for hs in halves:
+            nc.scalar.activation(tq[:, hs], ax[:, hs], ACT.Tanh, bias=poly[:, 2 * NT : 2 * NT + 1], scale=0.5)
+        for hs in halves:
+            nc.scalar.activation(qq[:, hs], tq[:, hs], ACT.Square, bias=c_half, scale=-0.5)
+        for hs in halves:
+            nc.vector.scalar_tensor_tensor(nn[:, hs], px[:, hs], rt[:], swb[:, hs], ALU.mult, ALU.mult)
+        for j, hs in enumerate(halves):
+            nc.vector.scalar_tensor_tensor(e1[:, hs], qq[:, hs], 1.0, nn[:, hs], ALU.mult, ALU.mult, accum_out=s[:, j : j + 1])
+        nc.vector.tensor_copy(s1[:].indirect(offsets[:]), e1[:])
+
+        c0 = sb.tile([P, NB], F32, name="c0")
+        cf = sb.tile([P, NB], F32, name="cf")
+        nc.scalar.activation(c0[:], kf[:], ACT.Copy, scale=s[:, 0:1])
+
+        def finish_factor(b):
+            nc.scalar.activation(cf[:, b : b + 1], s[:, 1:2], ACT.Identity, bias=c0[:, b : b + 1], scale=kf[:, b : b + 1])
+
+        cp = sb.tile([P, G_PIECES[-1][1]], F32, name="cp")
+        base = sb.tile([P, V], F32, name="base")
+        res = sb.tile([P, V], F32, name="res")
+        for lo, hi in G_PIECES:
+            b = lo // W
+            if lo % W == 0:
+                finish_factor(b)
+            nc.scalar.activation(cp[:, lo:hi], p[:, lo:hi], ACT.Copy, scale=cf[:, b : b + 1])
+            nc.gpsimd.tensor_tensor(base[:, lo:hi], cp[:, lo:hi], old_sb[:, lo:hi], ALU.add)
+        g_end = G_PIECES[-1][1]
+        for lo, hi in ((2 * W, 3 * W), (3 * W, V)):
+            b = lo // W
+            finish_factor(b)
+            nc.vector.scalar_tensor_tensor(base[:, lo:hi], p[:, lo:hi], cf[:, b : b + 1], old_sb[:, lo:hi], ALU.mult, ALU.add)
+        for lo, hi in ((g_end, 3 * W), (3 * W, V), (0, W), (W, W + 320), (W + 320, g_end)):
+            nc.vector.scalar_tensor_tensor(res[:, lo:hi], s1[:, lo:hi], 2.0, base[:, lo:hi], ALU.mult, ALU.add)
+            nc.sync.dma_start(out=out[:, lo:hi], in_=res[:, lo:hi])

@@ -1,6 +1,7 @@
 from contextlib import ExitStack
 
 import concourse.mybir as mybir
+from concourse.masks import make_identity
 
 D, V, Q, I = 512, 2048, 128, 512
 FLOPS = 2 * D * V * Q
@@ -26,7 +27,7 @@ TH_FLOOR = 2.0**-100
 LOG_DEN = 2520
 LOG_POLY = (-252, 2800, -14175, 43200, -88200, 127008, -132300, 100800, -56700, 25200, -7381)
 NT = len(LOG_POLY) - 1
-G_PIECES = ((0, 192), (192, 512), (512, 1024))
+NPE = 3
 
 
 def tile_attend_bpresence_heads_kernel(tc, hid, voc_words, voc_scales, th, sw, old, offs, out):
@@ -39,14 +40,13 @@ def tile_attend_bpresence_heads_kernel(tc, hid, voc_words, voc_scales, th, sw, o
         nc.sync.dma_start(out=hraw[:], in_=hid.rearrange("(p j) q -> p j q", j=4))
         planes = sb.tile([P, V], U8, name="planes", align_bytes=64)
         nc.gpsimd.memset(planes[:].bitcast(I32), 0)
-        words = []
-        for h in range(2):
-            wt = sb.tile([P, V], U8, name="words%d" % h, align_bytes=64)
-            words.append(wt)
-        nc.sync.dma_start(out=words[0][:].bitcast(I32), in_=voc_words[0][:, 0:V].bitcast(I32))
         for g in range(4):
             nc.sync.dma_start(out=planes[32 * g : 32 * g + 4, :].bitcast(I32), in_=voc_scales[0][4 * g : 4 * g + 4, :].bitcast(I32))
-        nc.sync.dma_start(out=words[1][:].bitcast(I32), in_=voc_words[0][:, V : 2 * V].bitcast(I32))
+        words_a = sb.tile([P, 2 * W], U8, name="words_a", align_bytes=64)
+        words_b = sb.tile([P, 2 * (V - W)], U8, name="words_b", align_bytes=64)
+        nc.sync.dma_start(out=words_a[:].bitcast(I32), in_=voc_words[0][:, 0 : 2 * W].bitcast(I32))
+        nc.sync.dma_start(out=words_b[:].bitcast(I32), in_=voc_words[0][:, 2 * W : 2 * V].bitcast(I32))
+        words = [words_a[:]] + [words_b[:, 2 * W * b : 2 * W * (b + 1)] for b in range(NB - 1)]
         offsets = sb.tile([P, I // 16], U16, name="offsets")
         nc.sync.dma_start(offsets[:], offs)
         th_raw = sb.tile([P, 1], F32, name="th_raw")
@@ -71,6 +71,8 @@ def tile_attend_bpresence_heads_kernel(tc, hid, voc_words, voc_scales, th, sw, o
         nc.gpsimd.memset(f[:, NB - 2 : NB], 1.0)
         s1 = sb.tile([P, V], F32, name="s1")
         nc.gpsimd.memset(s1[:, 0 : 2 * W], 0.0)
+        ident = sb.tile([P, P], F32, name="ident")
+        make_identity(nc, ident[:])
         nc.vector.memset(s1[:, 2 * W : 3 * W], 0.0)
         nc.vector.memset(s1[:, 3 * W : V], 0.0)
 
@@ -83,10 +85,10 @@ def tile_attend_bpresence_heads_kernel(tc, hid, voc_words, voc_scales, th, sw, o
         hscale = sb.tile([P, Q], U8, name="hscale", align_bytes=64)
         nc.vector.quantize_mx(out=codes[:].bitcast(FP8X4), scales=hscale[:], in_=grouped[:].rearrange("p q t -> p (q t)"))
 
-        swb = sb.tile([P, I], F32, name="swb", tag="early_a", align_bytes=64)
-        nc.sync.dma_start(out=swb[:], in_=sw[0].partition_broadcast(P))
-        old_sb = sb.tile([P, V], F32, name="old_sb", tag="early_b", align_bytes=64)
+        old_sb = sb.tile([P, V], F32, name="old_sb", tag="early_a", align_bytes=64)
         nc.sync.dma_start(out=old_sb[:], in_=old)
+        sw4 = sb.tile([P, 4], F32, name="sw4", tag="early_b", align_bytes=64)
+        nc.sync.dma_start(out=sw4[:], in_=sw[0].rearrange("(p c) -> p c", c=4))
 
         thc = sb.tile([P, 2], F32, name="thc")
         nc.vector.tensor_scalar(thc[:, 0:1], th_raw[:], TH_FLOOR, None, ALU.max)
@@ -102,13 +104,12 @@ def tile_attend_bpresence_heads_kernel(tc, hid, voc_words, voc_scales, th, sw, o
         unit = [1.0, 1.0, f[:, 2:3]]
         for b in range(NB):
             cols = slice(b * W, (b + 1) * W)
-            bank = ps.tile([P, W], F32, name="bank%d" % b)
-            wcol = (b % 2) * 2 * W
+            bank = ps.tile([P, W], F32, name="bank%d" % b, tag="bank%d" % b)
             nc.tensor.matmul_mx(
                 out=bank[:],
                 lhsT=codes[:].bitcast(FP8X4),
                 lhsT_scale=hscale[:],
-                rhs=words[b // 2][:, wcol : wcol + 2 * W].bitcast(FP4X4),
+                rhs=words[b].bitcast(FP4X4),
                 rhs_scale=planes[:, cols],
                 start=True,
                 stop=True,
@@ -121,6 +122,17 @@ def tile_attend_bpresence_heads_kernel(tc, hid, voc_words, voc_scales, th, sw, o
         nc.scalar.activation(f[:, 0 : NB - 1], m[:, 0 : NB - 1], ACT.Exp, bias=nmax[:])
         last = slice((NB - 1) * W, V)
         nc.scalar.activation(p[:, last], a[:, last], ACT.Exp, bias=nmax[:], scale=px[:, 0:1], accum_out=z[:, NB - 1 : NB])
+
+        swp = ps.tile([P, 4, P], F32, name="swp", tag="bank3")
+        for c in range(4):
+            nc.tensor.transpose(swp[:, c, :], sw4[:, c : c + 1].to_broadcast([P, P]), ident[:])
+        turned = []
+        for b in range(NPE):
+            tb = ps.tile([P, W], F32, name="turned%d" % b)
+            turned.append(tb)
+            for j in range(4):
+                lo = b * W + j * P
+                nc.tensor.matmul(tb[:, j * P : (j + 1) * P], old_sb[:, lo : lo + P], ident[:], start=(j == 0), stop=False, is_transpose=True)
 
         H = I // 2
         ax = sb.tile([P, I], F32, name="ax")
@@ -152,8 +164,15 @@ def tile_attend_bpresence_heads_kernel(tc, hid, voc_words, voc_scales, th, sw, o
             nc.scalar.activation(tq[:, hs], ax[:, hs], ACT.Tanh, bias=poly[:, 2 * NT : 2 * NT + 1], scale=0.5)
         for hs in halves:
             nc.scalar.activation(qq[:, hs], tq[:, hs], ACT.Square, bias=c_half, scale=-0.5)
-        for hs in halves:
-            nc.vector.scalar_tensor_tensor(nn[:, hs], px[:, hs], rt[:], swb[:, hs], ALU.mult, ALU.mult)
+        for j, hs in enumerate(halves):
+            nc.vector.scalar_tensor_tensor(
+                nn[:, hs].rearrange("m (k c) -> m k c", c=4),
+                px[:, hs].rearrange("m (k c) -> m k c", c=4),
+                rt[:],
+                swp[:].rearrange("m c k -> m k c")[:, 64 * j : 64 * (j + 1), :],
+                ALU.mult,
+                ALU.mult,
+            )
         for j, hs in enumerate(halves):
             nc.vector.scalar_tensor_tensor(e1[:, hs], qq[:, hs], 1.0, nn[:, hs], ALU.mult, ALU.mult, accum_out=s[:, j : j + 1])
         nc.vector.tensor_copy(s1[:].indirect(offsets[:]), e1[:])
@@ -165,20 +184,30 @@ def tile_attend_bpresence_heads_kernel(tc, hid, voc_words, voc_scales, th, sw, o
         def finish_factor(b):
             nc.scalar.activation(cf[:, b : b + 1], s[:, 1:2], ACT.Identity, bias=c0[:, b : b + 1], scale=kf[:, b : b + 1])
 
-        cp = sb.tile([P, G_PIECES[-1][1]], F32, name="cp")
-        base = sb.tile([P, V], F32, name="base")
-        res = sb.tile([P, V], F32, name="res")
-        for lo, hi in G_PIECES:
-            b = lo // W
-            if lo % W == 0:
-                finish_factor(b)
-            nc.scalar.activation(cp[:, lo:hi], p[:, lo:hi], ACT.Copy, scale=cf[:, b : b + 1])
-            nc.gpsimd.tensor_tensor(base[:, lo:hi], cp[:, lo:hi], old_sb[:, lo:hi], ALU.add)
-        g_end = G_PIECES[-1][1]
-        for lo, hi in ((2 * W, 3 * W), (3 * W, V)):
-            b = lo // W
+        cp = sb.tile([P, NPE * W], F32, name="cp")
+        for b in range(NPE):
             finish_factor(b)
-            nc.vector.scalar_tensor_tensor(base[:, lo:hi], p[:, lo:hi], cf[:, b : b + 1], old_sb[:, lo:hi], ALU.mult, ALU.add)
-        for lo, hi in ((g_end, 3 * W), (3 * W, V), (0, W), (W, W + 320), (W + 320, g_end)):
-            nc.vector.scalar_tensor_tensor(res[:, lo:hi], s1[:, lo:hi], 2.0, base[:, lo:hi], ALU.mult, ALU.add)
-            nc.sync.dma_start(out=out[:, lo:hi], in_=res[:, lo:hi])
+            nc.scalar.activation(cp[:, b * W : (b + 1) * W], p[:, b * W : (b + 1) * W], ACT.Copy, scale=cf[:, b : b + 1])
+            for j in range(4):
+                lo = b * W + j * P
+                nc.tensor.matmul(turned[b][:, j * P : (j + 1) * P], cp[:, lo : lo + P], ident[:], start=False, stop=(j == 3), is_transpose=True)
+        finish_factor(NB - 1)
+        base_t = sb.tile([P, NPE * W], F32, name="base_t")
+        bases = []
+        for b in range(NPE):
+            nc.scalar.copy(base_t[:, b * W : (b + 1) * W], turned[b][:])
+            bb = ps.tile([P, W], F32, name="base%d" % b, tag="bank%d" % b)
+            bases.append(bb)
+            for j in range(4):
+                lo = b * W + j * P
+                nc.tensor.transpose(bb[:, j * P : (j + 1) * P], base_t[:, lo : lo + P], ident[:])
+        base_v = sb.tile([P, W], F32, name="base_v")
+        bases.append(base_v)
+        res = sb.tile([P, V], F32, name="res")
+        for lo, hi in ((0, W // 2), (W // 2, W)):
+            cols = slice(NPE * W + lo, NPE * W + hi)
+            nc.vector.scalar_tensor_tensor(base_v[:, lo:hi], p[:, cols], cf[:, NPE : NPE + 1], old_sb[:, cols], ALU.mult, ALU.add)
+        for b, lo, hi in ((3, 0, 256), (3, 256, W), (0, 0, W), (1, 0, W), (2, 0, 320), (2, 320, W)):
+            cols = slice(b * W + lo, b * W + hi)
+            nc.vector.scalar_tensor_tensor(res[:, cols], s1[:, cols], 2.0, bases[b][:, lo:hi], ALU.mult, ALU.add)
+            nc.sync.dma_start(out=out[:, cols], in_=res[:, cols])

@@ -66,9 +66,13 @@ def tile_attend_bpresence_heads_kernel(tc, hid, voc_words, voc_scales, th, sw, o
         px = sb.tile([P, I], F32, name="px")
         c_shift = px[:, I - 1 : I]
         nc.vector.memset(c_shift, LOG_SHIFT)
-        nc.vector.memset(px[:, 0:1], 1.0)
+        H = I // 2
+        ax = sb.tile([P, I], F32, name="ax")
+        f_scale = ax[:, I - 1 : I]
+        nc.vector.memset(f_scale, -1.0)
+        minus = sb.tile([P, H], F32, name="minus")
+        nc.vector.memset(minus[:], -1.0)
         f = sb.tile([P, NB], F32, name="f")
-        nc.gpsimd.memset(f[:, NB - 2 : NB], 1.0)
         s1 = sb.tile([P, V], F32, name="s1")
         nc.gpsimd.memset(s1[:, 0 : 2 * W], 0.0)
         ident = sb.tile([P, P], F32, name="ident")
@@ -97,11 +101,9 @@ def tile_attend_bpresence_heads_kernel(tc, hid, voc_words, voc_scales, th, sw, o
 
         a = sb.tile([P, V], F32, name="a")
         p = sb.tile([P, V], F32, name="p")
-        m = sb.tile([P, NB], F32, name="m")
+        nm = sb.tile([P, NB], F32, name="nm")
         nmax = sb.tile([P, 1], F32, name="nmax")
         z = sb.tile([P, NB], F32, name="z")
-        nm = [f[:, 0:1], f[:, 1:2], z[:, NB - 1 : NB]]
-        unit = [1.0, 1.0, f[:, 2:3]]
         for b in range(NB):
             cols = slice(b * W, (b + 1) * W)
             bank = ps.tile([P, W], F32, name="bank%d" % b, tag="bank%d" % b)
@@ -114,14 +116,10 @@ def tile_attend_bpresence_heads_kernel(tc, hid, voc_words, voc_scales, th, sw, o
                 start=True,
                 stop=True,
             )
-            nc.vector.tensor_scalar(a[:, cols], bank[:], 1.0, None, ALU.mult, ALU.max, accum_out=m[:, b : b + 1])
-            if b < NB - 1:
-                nc.gpsimd.tensor_scalar(nm[b], m[:, b : b + 1], -1.0, 0.0, ALU.mult, ALU.add)
-                nc.scalar.activation(p[:, cols], a[:, cols], ACT.Exp, bias=nm[b], scale=unit[b], accum_out=z[:, b : b + 1])
-        nc.vector.tensor_reduce(nmax[:], m[:], AX.X, ALU.max, negate=True)
-        nc.scalar.activation(f[:, 0 : NB - 1], m[:, 0 : NB - 1], ACT.Exp, bias=nmax[:])
-        last = slice((NB - 1) * W, V)
-        nc.scalar.activation(p[:, last], a[:, last], ACT.Exp, bias=nmax[:], scale=px[:, 0:1], accum_out=z[:, NB - 1 : NB])
+            nc.vector.tensor_scalar(a[:, cols], bank[:], -1.0, None, ALU.mult, ALU.min, accum_out=nm[:, b : b + 1])
+            nc.scalar.activation(p[:, cols], a[:, cols], ACT.Exp, bias=nm[:, b : b + 1], scale=-1.0, accum_out=z[:, b : b + 1])
+        nc.vector.tensor_reduce(nmax[:], nm[:], AX.X, ALU.min)
+        nc.scalar.activation(f[:], nm[:], ACT.Exp, bias=nmax[:], scale=f_scale)
 
         swp = ps.tile([P, 4, P], F32, name="swp", tag="bank3")
         for c in range(4):
@@ -134,19 +132,18 @@ def tile_attend_bpresence_heads_kernel(tc, hid, voc_words, voc_scales, th, sw, o
                 lo = b * W + j * P
                 nc.tensor.matmul(tb[:, j * P : (j + 1) * P], old_sb[:, lo : lo + P], ident[:], start=(j == 0), stop=False, is_transpose=True)
 
-        H = I // 2
-        ax = sb.tile([P, I], F32, name="ax")
-        nc.vector.tensor_copy(ax[:], a[:].indirect(offsets[:]))
+        halves = (slice(0, H), slice(H, I))
+        nc.vector.tensor_tensor(ax[:, halves[0]], a[:].indirect(offsets[:, 0 : H // 16]), minus[:], ALU.mult)
         hb = sb.tile([P, 1], F32, name="hb")
         nc.vector.tensor_scalar(hb[:], nmax[:], 0.5, LOG_SHIFT / 2, ALU.mult, ALU.add)
         junk = sb.tile([P, NB], F32, name="junk")
         t = sb.tile([P, 1], F32, name="t")
-        halves = (slice(0, H), slice(H, I))
         nc.scalar.activation(px[:, halves[0]], ax[:, halves[0]], ACT.Exp, bias=nmax[:])
         nc.vector.scalar_tensor_tensor(junk[:], f[:], th1, z[:], ALU.mult, ALU.mult, accum_out=t[:])
+        nc.vector.tensor_tensor(ax[:, halves[1]], a[:].indirect(offsets[:, H // 16 : I // 16]), minus[:], ALU.mult)
         nc.scalar.activation(factor[:, 1 : 2 * NT : 2], t[:].bitcast(U32).to_broadcast([P, NT]), ACT.Exp, bias=c_shift, scale=-LOG_SLOPE)
-        nc.vector.tensor_copy(factor[:, 0 : 2 * NT : 2], t[:].to_broadcast([P, NT]))
-        nc.vector.tensor_scalar(addend[:, 2 * NT : 2 * NT + 1], t[:].bitcast(I32), -LOG_SLOPE / 2, hb[:], ALU.mult, ALU.add)
+        nc.scalar.activation(factor[:, 0 : 2 * NT : 2], t[:].to_broadcast([P, NT]), ACT.Copy)
+        nc.scalar.activation(addend[:, 2 * NT : 2 * NT + 1], t[:].bitcast(U32), ACT.Identity, bias=hb[:], scale=-LOG_SLOPE / 2)
         nc.scalar.activation(px[:, halves[1]], ax[:, halves[1]], ACT.Exp, bias=nmax[:])
         rt = sb.tile([P, 1], F32, name="rt")
         nc.vector.reciprocal(rt[:], t[:])

@@ -1,3 +1,4 @@
+import math
 from contextlib import ExitStack
 
 import concourse.mybir as mybir
@@ -19,15 +20,28 @@ ACT = mybir.ActivationFunctionType
 AX = mybir.AxisListType
 
 P = 128
-NB = 4
-W = V // NB
+PACK = 4
+LIST_ROWS = 16
+CHUNK = 512
+CHUNKS = V // CHUNK
+HALF = I // 2
+TURNED_CHUNKS = CHUNKS - 1
+PIECE = 256
+
 LOG_SLOPE = 11629080.0 / 2.0**47
 LOG_SHIFT = 88.0
-TH_FLOOR = 2.0**-100
+LOG_TERMS = 10
 LOG_DEN = 2520
-LOG_POLY = (-252, 2800, -14175, 43200, -88200, 127008, -132300, 100800, -56700, 25200, -7381)
-NT = len(LOG_POLY) - 1
-NPE = 3
+SCAN = 2 * LOG_TERMS + 1
+TH_FLOOR = 2.0**-100
+
+
+def log_coefficient(k):
+    total = 0
+    for j in range(max(k, 1), LOG_TERMS + 1):
+        choose = math.factorial(j) // (math.factorial(k) * math.factorial(j - k))
+        total = total - (-1) ** k * choose * (LOG_DEN // j)
+    return float(total)
 
 
 def tile_attend_bpresence_heads_kernel(tc, hid, voc_words, voc_scales, th, sw, old, offs, out):
@@ -36,175 +50,206 @@ def tile_attend_bpresence_heads_kernel(tc, hid, voc_words, voc_scales, th, sw, o
         sb = ctx.enter_context(tc.tile_pool(name="sb", bufs=1))
         ps = ctx.enter_context(tc.psum_pool(name="ps", bufs=1))
 
-        hraw = sb.tile([P, 4, Q], F32, name="hraw", tag="early_a", align_bytes=64)
-        nc.sync.dma_start(out=hraw[:], in_=hid.rearrange("(p j) q -> p j q", j=4))
-        planes = sb.tile([P, V], U8, name="planes", align_bytes=64)
-        nc.gpsimd.memset(planes[:].bitcast(I32), 0)
-        for g in range(4):
-            nc.sync.dma_start(out=planes[32 * g : 32 * g + 4, :].bitcast(I32), in_=voc_scales[0][4 * g : 4 * g + 4, :].bitcast(I32))
-        words_a = sb.tile([P, 2 * W], U8, name="words_a", align_bytes=64)
-        words_b = sb.tile([P, 2 * (V - W)], U8, name="words_b", align_bytes=64)
-        nc.sync.dma_start(out=words_a[:].bitcast(I32), in_=voc_words[0][:, 0 : 2 * W].bitcast(I32))
-        nc.sync.dma_start(out=words_b[:].bitcast(I32), in_=voc_words[0][:, 2 * W : 2 * V].bitcast(I32))
-        words = [words_a[:]] + [words_b[:, 2 * W * b : 2 * W * (b + 1)] for b in range(NB - 1)]
-        offsets = sb.tile([P, I // 16], U16, name="offsets")
+        hid_rows = sb.tile([P, PACK, Q], F32, name="hid_rows", tag="hid_then_old", align_bytes=64)
+        nc.sync.dma_start(out=hid_rows[:], in_=hid.rearrange("(p j) q -> p j q", j=PACK))
+        voc_plane = sb.tile([P, V], U8, name="voc_plane", align_bytes=64)
+        nc.gpsimd.memset(voc_plane[:].bitcast(I32), 0)
+        for quadrant in range(4):
+            nc.sync.dma_start(
+                out=voc_plane[32 * quadrant : 32 * quadrant + 4, :].bitcast(I32),
+                in_=voc_scales[0][4 * quadrant : 4 * quadrant + 4, :].bitcast(I32),
+            )
+        words_first = sb.tile([P, 2 * CHUNK], U8, name="words_first", align_bytes=64)
+        words_rest = sb.tile([P, 2 * (V - CHUNK)], U8, name="words_rest", align_bytes=64)
+        nc.sync.dma_start(out=words_first[:].bitcast(I32), in_=voc_words[0][:, 0 : 2 * CHUNK].bitcast(I32))
+        nc.sync.dma_start(out=words_rest[:].bitcast(I32), in_=voc_words[0][:, 2 * CHUNK : 2 * V].bitcast(I32))
+        words = [words_first[:]] + [words_rest[:, 2 * CHUNK * b : 2 * CHUNK * (b + 1)] for b in range(CHUNKS - 1)]
+        offsets = sb.tile([P, I // LIST_ROWS], U16, name="offsets")
         nc.sync.dma_start(offsets[:], offs)
         th_raw = sb.tile([P, 1], F32, name="th_raw")
         nc.sync.dma_start(out=th_raw[:], in_=th)
 
-        consts = sb.tile([P, 1], F32, name="consts")
-        nc.vector.memset(consts[:], 0.5)
-        c_half = consts[:, 0:1]
-        warm = sb.tile([P, 1], F32, name="warm")
-        nc.scalar.activation(warm[:], c_half, ACT.Exp)
-        addend = sb.tile([P, 2 * NT + 1], F32, name="addend")
-        factor = sb.tile([P, 2 * NT + 1], F32, name="factor")
-        nc.vector.memset(addend[:, 0 : 2 * NT], 0.0)
-        for j, c in enumerate(LOG_POLY[1:]):
-            nc.vector.memset(addend[:, 2 * j + 1 : 2 * j + 2], float(c))
-        nc.vector.tensor_scalar(factor[:, 2 * NT : 2 * NT + 1], c_half, -1.0 / LOG_DEN, None, ALU.mult)
+        one_half = sb.tile([P, 1], F32, name="one_half")
+        nc.vector.memset(one_half[:], 0.5)
+        addend = sb.tile([P, SCAN], F32, name="addend")
+        factor = sb.tile([P, SCAN], F32, name="factor")
+        nc.scalar.activation(factor[:, SCAN - 1 : SCAN], one_half[:], ACT.Identity, scale=-1.0 / LOG_DEN)
+        nc.vector.memset(addend[:, 0 : SCAN - 1], 0.0)
+        for step in range(LOG_TERMS):
+            nc.vector.memset(addend[:, 2 * step + 1 : 2 * step + 2], log_coefficient(LOG_TERMS - 1 - step))
         px = sb.tile([P, I], F32, name="px")
-        c_shift = px[:, I - 1 : I]
-        nc.vector.memset(c_shift, LOG_SHIFT)
-        H = I // 2
-        ax = sb.tile([P, I], F32, name="ax")
-        f_scale = ax[:, I - 1 : I]
-        nc.vector.memset(f_scale, -1.0)
-        minus = sb.tile([P, H], F32, name="minus")
-        nc.vector.memset(minus[:], -1.0)
-        f = sb.tile([P, NB], F32, name="f")
+        log_shift = px[:, I - 1 : I]
+        nc.vector.memset(log_shift, LOG_SHIFT)
+        listed = sb.tile([P, I], F32, name="listed")
+        minus_one = listed[:, I - 1 : I]
+        nc.vector.memset(minus_one, -1.0)
+        minus_ones = sb.tile([P, HALF], F32, name="minus_ones")
+        nc.vector.memset(minus_ones[:], -1.0)
         s1 = sb.tile([P, V], F32, name="s1")
-        nc.gpsimd.memset(s1[:, 0 : 2 * W], 0.0)
+        nc.gpsimd.memset(s1[:, 0 : 2 * CHUNK], 0.0)
         ident = sb.tile([P, P], F32, name="ident")
         make_identity(nc, ident[:])
-        nc.vector.memset(s1[:, 2 * W : 3 * W], 0.0)
-        nc.vector.memset(s1[:, 3 * W : V], 0.0)
+        nc.vector.memset(s1[:, 2 * CHUNK : 3 * CHUNK], 0.0)
+        nc.vector.memset(s1[:, 3 * CHUNK : V], 0.0)
 
-        grouped = sb.tile([P, Q, 4], BF16, name="grouped", tag="early_b", align_bytes=64)
+        grouped = sb.tile([P, Q, PACK], BF16, name="grouped", tag="grouped_then_sw", align_bytes=64)
         nc.vector.tensor_copy(
             out=grouped[:].rearrange("p (c i) t -> p c t i", i=4),
-            in_=hraw[:].rearrange("p t (c i) -> p c t i", i=4),
+            in_=hid_rows[:].rearrange("p t (c i) -> p c t i", i=4),
         )
-        codes = sb.tile([P, Q], U32, name="codes", align_bytes=64)
-        hscale = sb.tile([P, Q], U8, name="hscale", align_bytes=64)
-        nc.vector.quantize_mx(out=codes[:].bitcast(FP8X4), scales=hscale[:], in_=grouped[:].rearrange("p q t -> p (q t)"))
+        hid_codes = sb.tile([P, Q], U32, name="hid_codes", align_bytes=64)
+        hid_plane = sb.tile([P, Q], U8, name="hid_plane", align_bytes=64)
+        nc.vector.quantize_mx(out=hid_codes[:].bitcast(FP8X4), scales=hid_plane[:], in_=grouped[:].rearrange("p q t -> p (q t)"))
 
-        old_sb = sb.tile([P, V], F32, name="old_sb", tag="early_a", align_bytes=64)
+        old_sb = sb.tile([P, V], F32, name="old_sb", tag="hid_then_old", align_bytes=64)
         nc.sync.dma_start(out=old_sb[:], in_=old)
-        sw4 = sb.tile([P, 4], F32, name="sw4", tag="early_b", align_bytes=64)
-        nc.sync.dma_start(out=sw4[:], in_=sw[0].rearrange("(p c) -> p c", c=4))
+        sw_rows = sb.tile([P, 4], F32, name="sw_rows", tag="grouped_then_sw", align_bytes=64)
+        nc.sync.dma_start(out=sw_rows[:], in_=sw[0].rearrange("(k c) -> k c", c=4))
 
-        thc = sb.tile([P, 2], F32, name="thc")
-        nc.vector.tensor_scalar(thc[:, 0:1], th_raw[:], TH_FLOOR, None, ALU.max)
-        nc.vector.tensor_scalar(thc[:, 1:2], th_raw[:], TH_FLOOR, -2.0, ALU.max, ALU.mult)
-        th1, thm2 = thc[:, 0:1], thc[:, 1:2]
+        th_pair = sb.tile([P, 2], F32, name="th_pair")
+        th_safe, th_minus_two = th_pair[:, 0:1], th_pair[:, 1:2]
+        nc.vector.tensor_scalar(th_safe, th_raw[:], TH_FLOOR, None, ALU.max)
+        nc.vector.tensor_scalar(th_minus_two, th_raw[:], TH_FLOOR, -2.0, ALU.max, ALU.mult)
 
-        a = sb.tile([P, V], F32, name="a")
+        minus_a = sb.tile([P, V], F32, name="minus_a")
         p = sb.tile([P, V], F32, name="p")
-        nm = sb.tile([P, NB], F32, name="nm")
-        nmax = sb.tile([P, 1], F32, name="nmax")
-        z = sb.tile([P, NB], F32, name="z")
-        for b in range(NB):
-            cols = slice(b * W, (b + 1) * W)
-            bank = ps.tile([P, W], F32, name="bank%d" % b, tag="bank%d" % b)
+        minus_max = sb.tile([P, CHUNKS], F32, name="minus_max")
+        minus_m1 = sb.tile([P, 1], F32, name="minus_m1")
+        chunk_sum = sb.tile([P, CHUNKS], F32, name="chunk_sum")
+        chunk_factor = sb.tile([P, CHUNKS], F32, name="chunk_factor")
+        for b in range(CHUNKS):
+            cols = slice(b * CHUNK, (b + 1) * CHUNK)
+            scores = ps.tile([P, CHUNK], F32, name="scores%d" % b, tag="bank%d" % b)
             nc.tensor.matmul_mx(
-                out=bank[:],
-                lhsT=codes[:].bitcast(FP8X4),
-                lhsT_scale=hscale[:],
+                out=scores[:],
+                lhsT=hid_codes[:].bitcast(FP8X4),
+                lhsT_scale=hid_plane[:],
                 rhs=words[b].bitcast(FP4X4),
-                rhs_scale=planes[:, cols],
+                rhs_scale=voc_plane[:, cols],
                 start=True,
                 stop=True,
             )
-            nc.vector.tensor_scalar(a[:, cols], bank[:], -1.0, None, ALU.mult, ALU.min, accum_out=nm[:, b : b + 1])
-            nc.scalar.activation(p[:, cols], a[:, cols], ACT.Exp, bias=nm[:, b : b + 1], scale=-1.0, accum_out=z[:, b : b + 1])
-        nc.vector.tensor_reduce(nmax[:], nm[:], AX.X, ALU.min)
-        nc.scalar.activation(f[:], nm[:], ACT.Exp, bias=nmax[:], scale=f_scale)
+            nc.vector.tensor_scalar(minus_a[:, cols], scores[:], -1.0, None, ALU.mult, ALU.min, accum_out=minus_max[:, b : b + 1])
+            nc.scalar.activation(
+                p[:, cols], minus_a[:, cols], ACT.Exp, bias=minus_max[:, b : b + 1], scale=-1.0, accum_out=chunk_sum[:, b : b + 1]
+            )
+        nc.vector.tensor_reduce(minus_m1[:], minus_max[:], AX.X, ALU.min)
+        nc.scalar.activation(chunk_factor[:], minus_max[:], ACT.Exp, bias=minus_m1[:], scale=minus_one)
 
-        swp = ps.tile([P, 4, P], F32, name="swp", tag="bank3")
+        sw_all = ps.tile([P, 4, P], F32, name="sw_all", tag="bank%d" % (CHUNKS - 1))
         for c in range(4):
-            nc.tensor.transpose(swp[:, c, :], sw4[:, c : c + 1].to_broadcast([P, P]), ident[:])
-        turned = []
-        for b in range(NPE):
-            tb = ps.tile([P, W], F32, name="turned%d" % b)
-            turned.append(tb)
-            for j in range(4):
-                lo = b * W + j * P
-                nc.tensor.matmul(tb[:, j * P : (j + 1) * P], old_sb[:, lo : lo + P], ident[:], start=(j == 0), stop=False, is_transpose=True)
+            nc.tensor.transpose(sw_all[:, c, :], sw_rows[:, c : c + 1].to_broadcast([P, P]), ident[:])
 
-        halves = (slice(0, H), slice(H, I))
-        nc.vector.tensor_tensor(ax[:, halves[0]], a[:].indirect(offsets[:, 0 : H // 16]), minus[:], ALU.mult)
-        hb = sb.tile([P, 1], F32, name="hb")
-        nc.vector.tensor_scalar(hb[:], nmax[:], 0.5, LOG_SHIFT / 2, ALU.mult, ALU.add)
-        junk = sb.tile([P, NB], F32, name="junk")
+        def turn(dst, src, b, opens, closes):
+            blocks = CHUNK // P
+            for j in range(blocks):
+                first = b * CHUNK + j * P
+                nc.tensor.matmul(
+                    dst[:, j * P : (j + 1) * P],
+                    src[:, first : first + P],
+                    ident[:],
+                    start=(opens and j == 0),
+                    stop=(closes and j == blocks - 1),
+                    is_transpose=True,
+                )
+
+        turned = [ps.tile([P, CHUNK], F32, name="turned%d" % b) for b in range(TURNED_CHUNKS)]
+        for b in range(TURNED_CHUNKS):
+            turn(turned[b], old_sb, b, True, False)
+
+        halves = (slice(0, HALF), slice(HALF, I))
+
+        def look_up(h):
+            entries = offsets[:, h * HALF // LIST_ROWS : (h + 1) * HALF // LIST_ROWS]
+            nc.vector.tensor_tensor(listed[:, halves[h]], minus_a[:].indirect(entries), minus_ones[:], ALU.mult)
+
+        def listed_exp(h):
+            nc.scalar.activation(px[:, halves[h]], listed[:, halves[h]], ACT.Exp, bias=minus_m1[:])
+
+        look_up(0)
+        half_shift = sb.tile([P, 1], F32, name="half_shift")
+        nc.vector.tensor_scalar(half_shift[:], minus_m1[:], 0.5, LOG_SHIFT / 2, ALU.mult, ALU.add)
+        t_terms = sb.tile([P, CHUNKS], F32, name="t_terms")
         t = sb.tile([P, 1], F32, name="t")
-        nc.scalar.activation(px[:, halves[0]], ax[:, halves[0]], ACT.Exp, bias=nmax[:])
-        nc.vector.scalar_tensor_tensor(junk[:], f[:], th1, z[:], ALU.mult, ALU.mult, accum_out=t[:])
-        nc.vector.tensor_tensor(ax[:, halves[1]], a[:].indirect(offsets[:, H // 16 : I // 16]), minus[:], ALU.mult)
-        nc.scalar.activation(factor[:, 1 : 2 * NT : 2], t[:].bitcast(U32).to_broadcast([P, NT]), ACT.Exp, bias=c_shift, scale=-LOG_SLOPE)
-        nc.scalar.activation(factor[:, 0 : 2 * NT : 2], t[:].to_broadcast([P, NT]), ACT.Copy)
-        nc.scalar.activation(addend[:, 2 * NT : 2 * NT + 1], t[:].bitcast(U32), ACT.Identity, bias=hb[:], scale=-LOG_SLOPE / 2)
-        nc.scalar.activation(px[:, halves[1]], ax[:, halves[1]], ACT.Exp, bias=nmax[:])
-        rt = sb.tile([P, 1], F32, name="rt")
-        nc.vector.reciprocal(rt[:], t[:])
-        poly = sb.tile([P, 2 * NT + 1], F32, name="poly")
-        nc.vector.tensor_tensor_scan(poly[:], factor[:], addend[:], float(LOG_POLY[0]), ALU.mult, ALU.add)
-        kf = sb.tile([P, NB], F32, name="kf")
-        nc.vector.tensor_scalar(kf[:], f[:], rt[:], thm2, ALU.mult, ALU.mult)
+        listed_exp(0)
+        nc.vector.scalar_tensor_tensor(t_terms[:], chunk_factor[:], th_safe, chunk_sum[:], ALU.mult, ALU.mult, accum_out=t[:])
+        look_up(1)
+        t_bits = t[:].bitcast(U32)
+        nc.scalar.activation(factor[:, 1 : SCAN - 1 : 2], t_bits.to_broadcast([P, LOG_TERMS]), ACT.Exp, bias=log_shift, scale=-LOG_SLOPE)
+        nc.scalar.activation(factor[:, 0 : SCAN - 1 : 2], t[:].to_broadcast([P, LOG_TERMS]), ACT.Copy)
+        nc.scalar.activation(addend[:, SCAN - 1 : SCAN], t_bits, ACT.Identity, bias=half_shift[:], scale=-LOG_SLOPE / 2)
+        listed_exp(1)
+        inv_t = sb.tile([P, 1], F32, name="inv_t")
+        nc.vector.reciprocal(inv_t[:], t[:])
+        states = sb.tile([P, SCAN], F32, name="states")
+        nc.vector.tensor_tensor_scan(states[:], factor[:], addend[:], log_coefficient(LOG_TERMS), ALU.mult, ALU.add)
+        minus_half_c = states[:, SCAN - 1 : SCAN]
+        per_sum = sb.tile([P, CHUNKS], F32, name="per_sum")
+        nc.vector.tensor_scalar(per_sum[:], chunk_factor[:], inv_t[:], th_minus_two, ALU.mult, ALU.mult)
 
-        tq = sb.tile([P, I], F32, name="tq")
-        qq = sb.tile([P, I], F32, name="qq")
-        nn = sb.tile([P, I], F32, name="nn")
+        tanh = sb.tile([P, I], F32, name="tanh")
+        inv_square = sb.tile([P, I], F32, name="inv_square")
+        sw_w = sb.tile([P, I], F32, name="sw_w")
         e1 = sb.tile([P, I], F32, name="e1")
-        s = sb.tile([P, 2], F32, name="s")
-        for hs in halves:
-            nc.scalar.activation(tq[:, hs], ax[:, hs], ACT.Tanh, bias=poly[:, 2 * NT : 2 * NT + 1], scale=0.5)
-        for hs in halves:
-            nc.scalar.activation(qq[:, hs], tq[:, hs], ACT.Square, bias=c_half, scale=-0.5)
-        for j, hs in enumerate(halves):
+        e1_sum = sb.tile([P, 2], F32, name="e1_sum")
+        for slots in halves:
+            nc.scalar.activation(tanh[:, slots], listed[:, slots], ACT.Tanh, bias=minus_half_c, scale=0.5)
+        for slots in halves:
+            nc.scalar.activation(inv_square[:, slots], tanh[:, slots], ACT.Square, bias=one_half[:], scale=-0.5)
+        for h, slots in enumerate(halves):
             nc.vector.scalar_tensor_tensor(
-                nn[:, hs].rearrange("m (k c) -> m k c", c=4),
-                px[:, hs].rearrange("m (k c) -> m k c", c=4),
-                rt[:],
-                swp[:].rearrange("m c k -> m k c")[:, 64 * j : 64 * (j + 1), :],
+                sw_w[:, slots].rearrange("m (k c) -> m k c", c=4),
+                px[:, slots].rearrange("m (k c) -> m k c", c=4),
+                inv_t[:],
+                sw_all[:].rearrange("m c k -> m k c")[:, h * HALF // 4 : (h + 1) * HALF // 4, :],
                 ALU.mult,
                 ALU.mult,
             )
-        for j, hs in enumerate(halves):
-            nc.vector.scalar_tensor_tensor(e1[:, hs], qq[:, hs], 1.0, nn[:, hs], ALU.mult, ALU.mult, accum_out=s[:, j : j + 1])
+        for h, slots in enumerate(halves):
+            nc.vector.scalar_tensor_tensor(
+                e1[:, slots], inv_square[:, slots], 1.0, sw_w[:, slots], ALU.mult, ALU.mult, accum_out=e1_sum[:, h : h + 1]
+            )
         nc.vector.tensor_copy(s1[:].indirect(offsets[:]), e1[:])
 
-        c0 = sb.tile([P, NB], F32, name="c0")
-        cf = sb.tile([P, NB], F32, name="cf")
-        nc.scalar.activation(c0[:], kf[:], ACT.Copy, scale=s[:, 0:1])
+        first_part = sb.tile([P, CHUNKS], F32, name="first_part")
+        p_factor = sb.tile([P, CHUNKS], F32, name="p_factor")
+        nc.scalar.activation(first_part[:], per_sum[:], ACT.Copy, scale=e1_sum[:, 0:1])
 
         def finish_factor(b):
-            nc.scalar.activation(cf[:, b : b + 1], s[:, 1:2], ACT.Identity, bias=c0[:, b : b + 1], scale=kf[:, b : b + 1])
+            nc.scalar.activation(
+                p_factor[:, b : b + 1], e1_sum[:, 1:2], ACT.Identity, bias=first_part[:, b : b + 1], scale=per_sum[:, b : b + 1]
+            )
 
-        cp = sb.tile([P, NPE * W], F32, name="cp")
-        for b in range(NPE):
+        scaled_p = sb.tile([P, TURNED_CHUNKS * CHUNK], F32, name="scaled_p")
+        for b in range(TURNED_CHUNKS):
+            cols = slice(b * CHUNK, (b + 1) * CHUNK)
             finish_factor(b)
-            nc.scalar.activation(cp[:, b * W : (b + 1) * W], p[:, b * W : (b + 1) * W], ACT.Copy, scale=cf[:, b : b + 1])
-            for j in range(4):
-                lo = b * W + j * P
-                nc.tensor.matmul(turned[b][:, j * P : (j + 1) * P], cp[:, lo : lo + P], ident[:], start=False, stop=(j == 3), is_transpose=True)
-        finish_factor(NB - 1)
-        base_t = sb.tile([P, NPE * W], F32, name="base_t")
-        bases = []
-        for b in range(NPE):
-            nc.scalar.copy(base_t[:, b * W : (b + 1) * W], turned[b][:])
-            bb = ps.tile([P, W], F32, name="base%d" % b, tag="bank%d" % b)
-            bases.append(bb)
-            for j in range(4):
-                lo = b * W + j * P
-                nc.tensor.transpose(bb[:, j * P : (j + 1) * P], base_t[:, lo : lo + P], ident[:])
-        base_v = sb.tile([P, W], F32, name="base_v")
-        bases.append(base_v)
-        res = sb.tile([P, V], F32, name="res")
-        for lo, hi in ((0, W // 2), (W // 2, W)):
-            cols = slice(NPE * W + lo, NPE * W + hi)
-            nc.vector.scalar_tensor_tensor(base_v[:, lo:hi], p[:, cols], cf[:, NPE : NPE + 1], old_sb[:, cols], ALU.mult, ALU.add)
-        for b, lo, hi in ((3, 0, 256), (3, 256, W), (0, 0, W), (1, 0, W), (2, 0, 320), (2, 320, W)):
-            cols = slice(b * W + lo, b * W + hi)
-            nc.vector.scalar_tensor_tensor(res[:, cols], s1[:, cols], 2.0, bases[b][:, lo:hi], ALU.mult, ALU.add)
-            nc.sync.dma_start(out=out[:, cols], in_=res[:, cols])
+            nc.scalar.activation(scaled_p[:, cols], p[:, cols], ACT.Copy, scale=p_factor[:, b : b + 1])
+            turn(turned[b], scaled_p, b, False, True)
+        finish_factor(TURNED_CHUNKS)
+        base_turned = sb.tile([P, TURNED_CHUNKS * CHUNK], F32, name="base_turned")
+        base = []
+        for b in range(TURNED_CHUNKS):
+            nc.scalar.copy(base_turned[:, b * CHUNK : (b + 1) * CHUNK], turned[b][:])
+            base.append(ps.tile([P, CHUNK], F32, name="base%d" % b, tag="bank%d" % b))
+            for j in range(CHUNK // P):
+                first = b * CHUNK + j * P
+                nc.tensor.transpose(base[b][:, j * P : (j + 1) * P], base_turned[:, first : first + P], ident[:])
+        base.append(sb.tile([P, CHUNK], F32, name="base_last"))
+        for first in range(0, CHUNK, PIECE):
+            cols = slice(TURNED_CHUNKS * CHUNK + first, TURNED_CHUNKS * CHUNK + first + PIECE)
+            nc.vector.scalar_tensor_tensor(
+                base[TURNED_CHUNKS][:, first : first + PIECE],
+                p[:, cols],
+                p_factor[:, TURNED_CHUNKS : TURNED_CHUNKS + 1],
+                old_sb[:, cols],
+                ALU.mult,
+                ALU.add,
+            )
+
+        result = sb.tile([P, V], F32, name="result")
+        for b in [TURNED_CHUNKS] + list(range(TURNED_CHUNKS)):
+            for first in range(0, CHUNK, PIECE):
+                cols = slice(b * CHUNK + first, b * CHUNK + first + PIECE)
+                nc.vector.scalar_tensor_tensor(result[:, cols], s1[:, cols], 2.0, base[b][:, first : first + PIECE], ALU.mult, ALU.add)
+                nc.sync.dma_start(out=out[:, cols], in_=result[:, cols])

import math
from contextlib import ExitStack

import concourse.mybir as mybir
from concourse.masks import make_identity

D, V, Q, I = 512, 2048, 128, 512
FLOPS = 2 * D * V * Q

F32 = mybir.dt.float32
BF16 = mybir.dt.bfloat16
I32 = mybir.dt.int32
U32 = mybir.dt.uint32
U16 = mybir.dt.uint16
U8 = mybir.dt.uint8
FP8X4 = mybir.dt.float8_e4m3fn_x4
FP4X4 = mybir.dt.float4_e2m1fn_x4
ALU = mybir.AluOpType
ACT = mybir.ActivationFunctionType
AX = mybir.AxisListType

P = 128
PACK = 4
LIST_ROWS = 16
CHUNK = 512
CHUNKS = V // CHUNK
HALF = I // 2
TURNED_CHUNKS = CHUNKS - 1
PIECE = 256

LOG_SLOPE = 11629080.0 / 2.0**47
LOG_SHIFT = 88.0
LOG_TERMS = 10
LOG_DEN = 2520
SCAN = 2 * LOG_TERMS + 1
TH_FLOOR = 2.0**-100


def log_coefficient(k):
    total = 0
    for j in range(max(k, 1), LOG_TERMS + 1):
        choose = math.factorial(j) // (math.factorial(k) * math.factorial(j - k))
        total = total - (-1) ** k * choose * (LOG_DEN // j)
    return float(total)


def tile_attend_bpresence_heads_kernel(tc, hid, voc_words, voc_scales, th, sw, old, offs, out):
    nc = tc.nc
    with ExitStack() as ctx:
        sb = ctx.enter_context(tc.tile_pool(name="sb", bufs=1))
        ps = ctx.enter_context(tc.psum_pool(name="ps", bufs=1))

        hid_rows = sb.tile([P, PACK, Q], F32, name="hid_rows", tag="hid_then_old", align_bytes=64)
        nc.sync.dma_start(out=hid_rows[:], in_=hid.rearrange("(p j) q -> p j q", j=PACK))
        voc_plane = sb.tile([P, V], U8, name="voc_plane", align_bytes=64)
        nc.gpsimd.memset(voc_plane[:].bitcast(I32), 0)
        for quadrant in range(4):
            nc.sync.dma_start(
                out=voc_plane[32 * quadrant : 32 * quadrant + 4, :].bitcast(I32),
                in_=voc_scales[0][4 * quadrant : 4 * quadrant + 4, :].bitcast(I32),
            )
        words_first = sb.tile([P, 2 * CHUNK], U8, name="words_first", align_bytes=64)
        words_rest = sb.tile([P, 2 * (V - CHUNK)], U8, name="words_rest", align_bytes=64)
        nc.sync.dma_start(out=words_first[:].bitcast(I32), in_=voc_words[0][:, 0 : 2 * CHUNK].bitcast(I32))
        nc.sync.dma_start(out=words_rest[:].bitcast(I32), in_=voc_words[0][:, 2 * CHUNK : 2 * V].bitcast(I32))
        words = [words_first[:]] + [words_rest[:, 2 * CHUNK * b : 2 * CHUNK * (b + 1)] for b in range(CHUNKS - 1)]
        offsets = sb.tile([P, I // LIST_ROWS], U16, name="offsets")
        nc.sync.dma_start(offsets[:], offs)
        th_raw = sb.tile([P, 1], F32, name="th_raw")
        nc.sync.dma_start(out=th_raw[:], in_=th)

        one_half = sb.tile([P, 1], F32, name="one_half")
        nc.vector.memset(one_half[:], 0.5)
        addend = sb.tile([P, SCAN], F32, name="addend")
        factor = sb.tile([P, SCAN], F32, name="factor")
        nc.scalar.activation(factor[:, SCAN - 1 : SCAN], one_half[:], ACT.Identity, scale=-1.0 / LOG_DEN)
        nc.vector.memset(addend[:, 0 : SCAN - 1], 0.0)
        for step in range(LOG_TERMS):
            nc.vector.memset(addend[:, 2 * step + 1 : 2 * step + 2], log_coefficient(LOG_TERMS - 1 - step))
        px = sb.tile([P, I], F32, name="px")
        log_shift = px[:, I - 1 : I]
        nc.vector.memset(log_shift, LOG_SHIFT)
        listed = sb.tile([P, I], F32, name="listed")
        minus_one = listed[:, I - 1 : I]
        nc.vector.memset(minus_one, -1.0)
        minus_ones = sb.tile([P, HALF], F32, name="minus_ones")
        nc.vector.memset(minus_ones[:], -1.0)
        s1 = sb.tile([P, V], F32, name="s1")
        nc.gpsimd.memset(s1[:, 0 : 2 * CHUNK], 0.0)
        ident = sb.tile([P, P], F32, name="ident")
        make_identity(nc, ident[:])
        nc.vector.memset(s1[:, 2 * CHUNK : 3 * CHUNK], 0.0)
        nc.vector.memset(s1[:, 3 * CHUNK : V], 0.0)

        grouped = sb.tile([P, Q, PACK], BF16, name="grouped", tag="grouped_then_sw", align_bytes=64)
        nc.vector.tensor_copy(
            out=grouped[:].rearrange("p (c i) t -> p c t i", i=4),
            in_=hid_rows[:].rearrange("p t (c i) -> p c t i", i=4),
        )
        hid_codes = sb.tile([P, Q], U32, name="hid_codes", align_bytes=64)
        hid_plane = sb.tile([P, Q], U8, name="hid_plane", align_bytes=64)
        nc.vector.quantize_mx(out=hid_codes[:].bitcast(FP8X4), scales=hid_plane[:], in_=grouped[:].rearrange("p q t -> p (q t)"))

        old_sb = sb.tile([P, V], F32, name="old_sb", tag="hid_then_old", align_bytes=64)
        nc.sync.dma_start(out=old_sb[:], in_=old)
        sw_rows = sb.tile([P, 4], F32, name="sw_rows", tag="grouped_then_sw", align_bytes=64)
        nc.sync.dma_start(out=sw_rows[:], in_=sw[0].rearrange("(k c) -> k c", c=4))

        th_pair = sb.tile([P, 2], F32, name="th_pair")
        th_safe, th_minus_two = th_pair[:, 0:1], th_pair[:, 1:2]
        nc.vector.tensor_scalar(th_safe, th_raw[:], TH_FLOOR, None, ALU.max)
        nc.vector.tensor_scalar(th_minus_two, th_raw[:], TH_FLOOR, -2.0, ALU.max, ALU.mult)

        minus_a = sb.tile([P, V], F32, name="minus_a")
        p = sb.tile([P, V], F32, name="p")
        minus_max = sb.tile([P, CHUNKS], F32, name="minus_max")
        minus_m1 = sb.tile([P, 1], F32, name="minus_m1")
        chunk_sum = sb.tile([P, CHUNKS], F32, name="chunk_sum")
        chunk_factor = sb.tile([P, CHUNKS], F32, name="chunk_factor")
        for b in range(CHUNKS):
            cols = slice(b * CHUNK, (b + 1) * CHUNK)
            scores = ps.tile([P, CHUNK], F32, name="scores%d" % b, tag="bank%d" % b)
            nc.tensor.matmul_mx(
                out=scores[:],
                lhsT=hid_codes[:].bitcast(FP8X4),
                lhsT_scale=hid_plane[:],
                rhs=words[b].bitcast(FP4X4),
                rhs_scale=voc_plane[:, cols],
                start=True,
                stop=True,
            )
            nc.vector.tensor_scalar(minus_a[:, cols], scores[:], -1.0, None, ALU.mult, ALU.min, accum_out=minus_max[:, b : b + 1])
            nc.scalar.activation(
                p[:, cols], minus_a[:, cols], ACT.Exp, bias=minus_max[:, b : b + 1], scale=-1.0, accum_out=chunk_sum[:, b : b + 1]
            )
        nc.vector.tensor_reduce(minus_m1[:], minus_max[:], AX.X, ALU.min)
        nc.scalar.activation(chunk_factor[:], minus_max[:], ACT.Exp, bias=minus_m1[:], scale=minus_one)

        sw_all = ps.tile([P, 4, P], F32, name="sw_all", tag="bank%d" % (CHUNKS - 1))
        for c in range(4):
            nc.tensor.transpose(sw_all[:, c, :], sw_rows[:, c : c + 1].to_broadcast([P, P]), ident[:])

        def turn(dst, src, b, opens, closes):
            blocks = CHUNK // P
            for j in range(blocks):
                first = b * CHUNK + j * P
                nc.tensor.matmul(
                    dst[:, j * P : (j + 1) * P],
                    src[:, first : first + P],
                    ident[:],
                    start=(opens and j == 0),
                    stop=(closes and j == blocks - 1),
                    is_transpose=True,
                )

        turned = [ps.tile([P, CHUNK], F32, name="turned%d" % b) for b in range(TURNED_CHUNKS)]
        for b in range(TURNED_CHUNKS):
            turn(turned[b], old_sb, b, True, False)

        halves = (slice(0, HALF), slice(HALF, I))

        def look_up(h):
            entries = offsets[:, h * HALF // LIST_ROWS : (h + 1) * HALF // LIST_ROWS]
            nc.vector.tensor_tensor(listed[:, halves[h]], minus_a[:].indirect(entries), minus_ones[:], ALU.mult)

        def listed_exp(h):
            nc.scalar.activation(px[:, halves[h]], listed[:, halves[h]], ACT.Exp, bias=minus_m1[:])

        look_up(0)
        half_shift = sb.tile([P, 1], F32, name="half_shift")
        nc.vector.tensor_scalar(half_shift[:], minus_m1[:], 0.5, LOG_SHIFT / 2, ALU.mult, ALU.add)
        t_terms = sb.tile([P, CHUNKS], F32, name="t_terms")
        t = sb.tile([P, 1], F32, name="t")
        listed_exp(0)
        nc.vector.scalar_tensor_tensor(t_terms[:], chunk_factor[:], th_safe, chunk_sum[:], ALU.mult, ALU.mult, accum_out=t[:])
        look_up(1)
        t_bits = t[:].bitcast(U32)
        nc.scalar.activation(factor[:, 1 : SCAN - 1 : 2], t_bits.to_broadcast([P, LOG_TERMS]), ACT.Exp, bias=log_shift, scale=-LOG_SLOPE)
        nc.scalar.activation(factor[:, 0 : SCAN - 1 : 2], t[:].to_broadcast([P, LOG_TERMS]), ACT.Copy)
        nc.scalar.activation(addend[:, SCAN - 1 : SCAN], t_bits, ACT.Identity, bias=half_shift[:], scale=-LOG_SLOPE / 2)
        listed_exp(1)
        inv_t = sb.tile([P, 1], F32, name="inv_t")
        nc.vector.reciprocal(inv_t[:], t[:])
        states = sb.tile([P, SCAN], F32, name="states")
        nc.vector.tensor_tensor_scan(states[:], factor[:], addend[:], log_coefficient(LOG_TERMS), ALU.mult, ALU.add)
        minus_half_c = states[:, SCAN - 1 : SCAN]
        per_sum = sb.tile([P, CHUNKS], F32, name="per_sum")
        nc.vector.tensor_scalar(per_sum[:], chunk_factor[:], inv_t[:], th_minus_two, ALU.mult, ALU.mult)

        tanh = sb.tile([P, I], F32, name="tanh")
        inv_square = sb.tile([P, I], F32, name="inv_square")
        sw_w = sb.tile([P, I], F32, name="sw_w")
        e1 = sb.tile([P, I], F32, name="e1")
        e1_sum = sb.tile([P, 2], F32, name="e1_sum")
        for slots in halves:
            nc.scalar.activation(tanh[:, slots], listed[:, slots], ACT.Tanh, bias=minus_half_c, scale=0.5)
        for slots in halves:
            nc.scalar.activation(inv_square[:, slots], tanh[:, slots], ACT.Square, bias=one_half[:], scale=-0.5)
        for h, slots in enumerate(halves):
            nc.vector.scalar_tensor_tensor(
                sw_w[:, slots].rearrange("m (k c) -> m k c", c=4),
                px[:, slots].rearrange("m (k c) -> m k c", c=4),
                inv_t[:],
                sw_all[:].rearrange("m c k -> m k c")[:, h * HALF // 4 : (h + 1) * HALF // 4, :],
                ALU.mult,
                ALU.mult,
            )
        for h, slots in enumerate(halves):
            nc.vector.scalar_tensor_tensor(
                e1[:, slots], inv_square[:, slots], 1.0, sw_w[:, slots], ALU.mult, ALU.mult, accum_out=e1_sum[:, h : h + 1]
            )
        nc.vector.tensor_copy(s1[:].indirect(offsets[:]), e1[:])

        first_part = sb.tile([P, CHUNKS], F32, name="first_part")
        p_factor = sb.tile([P, CHUNKS], F32, name="p_factor")
        nc.scalar.activation(first_part[:], per_sum[:], ACT.Copy, scale=e1_sum[:, 0:1])

        def finish_factor(b):
            nc.scalar.activation(
                p_factor[:, b : b + 1], e1_sum[:, 1:2], ACT.Identity, bias=first_part[:, b : b + 1], scale=per_sum[:, b : b + 1]
            )

        scaled_p = sb.tile([P, TURNED_CHUNKS * CHUNK], F32, name="scaled_p")
        for b in range(TURNED_CHUNKS):
            cols = slice(b * CHUNK, (b + 1) * CHUNK)
            finish_factor(b)
            nc.scalar.activation(scaled_p[:, cols], p[:, cols], ACT.Copy, scale=p_factor[:, b : b + 1])
            turn(turned[b], scaled_p, b, False, True)
        finish_factor(TURNED_CHUNKS)
        base_turned = sb.tile([P, TURNED_CHUNKS * CHUNK], F32, name="base_turned")
        base = []
        for b in range(TURNED_CHUNKS):
            nc.scalar.copy(base_turned[:, b * CHUNK : (b + 1) * CHUNK], turned[b][:])
            base.append(ps.tile([P, CHUNK], F32, name="base%d" % b, tag="bank%d" % b))
            for j in range(CHUNK // P):
                first = b * CHUNK + j * P
                nc.tensor.transpose(base[b][:, j * P : (j + 1) * P], base_turned[:, first : first + P], ident[:])
        base.append(sb.tile([P, CHUNK], F32, name="base_last"))
        for first in range(0, CHUNK, PIECE):
            cols = slice(TURNED_CHUNKS * CHUNK + first, TURNED_CHUNKS * CHUNK + first + PIECE)
            nc.vector.scalar_tensor_tensor(
                base[TURNED_CHUNKS][:, first : first + PIECE],
                p[:, cols],
                p_factor[:, TURNED_CHUNKS : TURNED_CHUNKS + 1],
                old_sb[:, cols],
                ALU.mult,
                ALU.add,
            )

        result = sb.tile([P, V], F32, name="result")
        for b in [TURNED_CHUNKS] + list(range(TURNED_CHUNKS)):
            for first in range(0, CHUNK, PIECE):
                cols = slice(b * CHUNK + first, b * CHUNK + first + PIECE)
                nc.vector.scalar_tensor_tensor(result[:, cols], s1[:, cols], 2.0, base[b][:, first : first + PIECE], ALU.mult, ALU.add)
                nc.sync.dma_start(out=out[:, cols], in_=result[:, cols])
